import numpy as np
CORES = [2,3,6,7,58,59,62,63,114,115,118,119]
N = 12
R, B, K = 4096, 128, 4
T = B * K
CAPP = 128
def entries(a): return a.T.reshape(-1)
def pack(v, P): return np.ascontiguousarray(np.asarray(v, np.int32).reshape(-1, P).T)
def lists(rng, how):
    I = rng.integers(0, N * R, (N, T))
    O = np.stack([rng.permutation(np.repeat(np.arange(N), CAPP))[:T] for r in range(N)])
    if how == "full": O = np.stack([rng.permutation(np.repeat(rng.permutation(N)[:T // CAPP], CAPP)) for r in range(N)])
    I = R * O + rng.integers(0, R, (N, T))
    if how == "alike": I = R * O + rng.integers(0, R, (N, 1))
    if how == "edge": I = R * O + np.where(rng.random((N, T)) < 0.5, 0, R - 1)
    if how == "sorted": I = np.sort(I, axis=1)
    return {"idx": np.stack([pack(I[r], 16) for r in range(N)])}
def setup_inputs(rng):
    return dict({"tab": rng.standard_normal((N, 128, R), dtype=np.float32)}, **lists(rng, "uniform"))
def setup_inputs_alike(rng):
    d = setup_inputs(rng); d.update(lists(rng, "alike"))
    for k in ("tab",): d[k] = (d[k].astype(np.float32) * 1024.0).astype(d[k].dtype)
    return d
def setup_inputs_edge(rng):
    d = setup_inputs(rng); d.update(lists(rng, "edge"))
    for k in ("tab",): d[k] = (d[k].astype(np.float32) * (1 / 1024.0)).astype(d[k].dtype)
    return d
def setup_inputs_full(rng):
    d = setup_inputs(rng); d.update(lists(rng, "full"))
    return d
def setup_inputs_sorted(rng):
    d = setup_inputs(rng); d.update(lists(rng, "sorted"))
    return d
def check_inputs(x):
    bad = []
    if x["idx"].min() < 0 or x["idx"].max() >= N * R: bad.append("idx out of range")
    if max(int(np.bincount(entries(a) // R, minlength=N).max()) for a in x["idx"]) > CAPP: bad.append("more than CAPP entries of a list point into one rank's part")
    return bad
def reference(tab, idx):
    A = np.concatenate(list(tab), axis=1).astype(np.float64)
    return {"y": np.stack([A[:, entries(idx[r])].reshape(128, B, K).sum(axis=2) for r in range(N)]).astype(np.float32)}

from concourse.bass import DstId, RemoteDMATransfer
from concourse.mybir import AluOpType, ActivationFunctionType

N = 12
R = 4096
B = 128
PAD = 4
WINC = R + 2 * PAD
LW = 32
SPLIT = 2048

SCRATCH = {
    "win": ("sbuf", [128, WINC], "float32"),
    "zi": ("sbuf", [128, LW], "int32"),
    "zf": ("sbuf", [128, LW], "float32"),
    "ramp": ("sbuf", [128, 128], "float32"),
    "rep": ("sbuf", [128, 128], "float32"),
    "land": ("sbuf", [128, N * LW], "uint16"),
    "off": ("sbuf", [128, N * LW], "uint16"),
    "ab": ("sbuf", [128, N * 2 * B], "float32"),
    "cd": ("sbuf", [128, N * 2 * B], "float32"),
    "rx": ("sbuf", [128, 9 * B], "float32"),
    "rxo": ("sbuf", [128, 2 * B], "float32"),
    "ysb": ("sbuf", [128, B], "float32"),
    "ps": ("psum", [128, 512], "float32"),
    "acc": ("psum", [128, 512], "float32"),
}
SEMAPHORES = ["idx", "tab", "pad", "iota", "rep", "zf", "mm", "own", "sent", "lista", "listb", "listn", "off", "ab",
              "cd", "rx0", "rx1", "rx2", "rx3", "o0", "o1", "loc", "acc", "fin", "y"]


def _bits(mask):
    return [e for e in range(16) if (mask >> e) & 1]


def _mask(engines):
    m = 0
    for e in engines:
        m |= 1 << e
    return m


def _layout(T, topo):
    chips = []
    for c in T.cores:
        if topo.chip(c) not in chips:
            chips.append(topo.chip(c))
    mem = [sorted([c for c in T.cores if topo.chip(c) == ch], key=lambda c: (topo.die(c), c)) for ch in chips]
    return chips, mem


def _order(x, j, nch, m):
    o = []
    for t in range(1, nch):
        for d in range(1, m):
            o.append(((x + t) % nch, (j + d) % m))
    for t in range(1, nch):
        o.append(((x + t) % nch, j))
    for d in range(1, m):
        o.append((x, (j + d) % m))
    o.append((x, j))
    return o


def rank_program(g, core, T, topo):
    rank = T.rank_of(core)
    if rank is None:
        return
    S = T.sem
    chips, mem = _layout(T, topo)
    nch, m = len(chips), len(mem[0])
    x = chips.index(topo.chip(core))
    j = mem[x].index(core)
    order = _order(x, j, nch, m)
    pos = {xy: p for p, xy in enumerate(order)}
    own = pos[(x, j)]

    def dst_id(c):
        rid, pid, _se = topo.addr(c)
        return DstId(rid=rid, pnc=pid)

    peers = [mem[x][(j + d) % m] for d in range(1, m)]
    far_a = mem[(x - 1) % nch]
    far_b = mem[(x + 1) % nch]
    off_e = _bits(topo.mask(core, far_a[0]))
    on_all = _bits(topo.mask(core, peers[0]))
    on_only = [e for e in on_all if e not in off_e]
    half = len(on_only) // 2
    pool = on_only + off_e[len(off_e) // 2:]
    quarter = [pool[4 * d:4 * d + 4] for d in range(m - 1)]

    win = T.win[:, 0:WINC]

    for k in range(4):
        q = g.sync if k < 2 else g.scalar
        q.dma_start(T.zi[0:16, 8 * k:8 * k + 8], T.idx[k::4, :]).then_inc(S.idx, 16)
    g.sync.dma_start(T.win[:, PAD:PAD + SPLIT], T.tab[:, 0:SPLIT]).then_inc(S.tab, 16)
    g.sync.wait_ge(S.sent, 1)
    g.sync.dma_start(T.win[:, PAD + SPLIT:PAD + R], T.tab[:, SPLIT:R]).then_inc(S.tab, 16)

    g.iota(T.ramp[0:16, :], [[0, 8], [1, 16]], 0, -1, allow_small_or_imprecise_dtypes=True).then_inc(S.iota, 1)
    v = g.vector
    v.memset(T.win[:, 0:PAD], 0.0).then_inc(S.pad, 1)
    v.memset(T.win[:, PAD + R:WINC], 0.0).then_inc(S.pad, 1)
    v.wait_ge(S.iota, 1)
    v.tensor_scalar(T.rep[0:16, :], T.ramp[0:16, :], 0.0, None, AluOpType.is_equal).then_inc(S.rep, 1)
    v.wait_ge(S.idx, 64)
    v.tensor_copy(T.zf[0:16, :], T.zi[0:16, :]).then_inc(S.zf, 1)
    g.tensor.wait_ge(S.rep, 1)
    g.tensor.wait_ge(S.zf, 1)
    g.tensor.matmul(T.ps[:, 0:LW], T.rep[0:16, :], T.zf[0:16, :], True, True).then_inc(S.mm, 1)
    v.wait_ge(S.mm, 1)
    v.tensor_copy(T.land[:, LW * own:LW * own + LW], T.ps[:, 0:LW]).then_inc(S.own, 1)

    def slot_at(c):
        xo = chips.index(topo.chip(c))
        jo = mem[xo].index(c)
        return _order(xo, jo, nch, m).index((x, j))

    def send_list(dests, engines, sem):
        g.remote_dma_fused([RemoteDMATransfer(
            dst_ids=[dst_id(c) for c in dests], dma_engine_mask=_mask(engines), remote_sem=sem,
            srcs=[T.land[:, LW * own:LW * own + LW]],
            dsts=[T.land[:, LW * slot_at(c):LW * slot_at(c) + LW] for c in dests], alu_op=0)], local_sem=S.loc)
        return len(engines)

    loc = 0
    g.wait_ge(S.own, 1)
    loc += send_list(far_a, off_e, S.lista)
    loc += send_list(far_b, off_e, S.listb)
    g.sem_inc(S.sent, 1)
    loc += send_list(peers, on_only, S.listn)

    n_a = m - 1
    n_fw = (nch - 1) * (m - 1)
    n_far = (nch - 1) * m

    def offsets(p0, p1):
        v.tensor_scalar(T.off[:, LW * p0:LW * p1], T.land[:, LW * p0:LW * p1], float(PAD - R * rank), float(PAD + R),
                        AluOpType.add, AluOpType.min).then_inc(S.off, 1)

    v.wait_ge(S.lista, m * len(off_e))
    offsets(0, n_a)

    for q in (g.scalar, v):
        q.wait_ge(S.off, 1)
        q.wait_ge(S.pad, 2)
        q.wait_ge(S.tab, 32)
    for p in range(N):
        if p == n_a - 1:
            v.wait_ge(S.listb, m * len(off_e))
            offsets(n_a, n_far)
        if p == n_a:
            g.scalar.wait_ge(S.off, 2)
            v.wait_ge(S.off, 2)
        if p == n_fw:
            v.wait_ge(S.listn, len(peers) * len(on_only))
            v.wait_ge(S.own, 1)
            offsets(n_far, N)
        if p == n_far:
            g.scalar.wait_ge(S.off, 3)
            v.wait_ge(S.off, 3)
        g.scalar.activation(T.ab[:, 2 * B * p:2 * B * p + 2 * B], win.indirect(T.off[:, LW * p:LW * p + 16]),
                            ActivationFunctionType.Copy).then_inc(S.ab, 1)
        v.tensor_copy(T.cd[:, 2 * B * p:2 * B * p + 2 * B],
                      win.indirect(T.off[:, LW * p + 16:LW * p + 32])).then_inc(S.cd, 1)

    def pieces(p):
        return [t[:, 2 * B * p + B * h:2 * B * p + B * h + B] for t in (T.ab, T.cd) for h in (0, 1)]

    def gathered(k):
        g.wait_ge(S.ab, k)
        g.wait_ge(S.cd, k)

    def rx_slot(t, d):
        return t * (m - 1) + (m - d - 1)

    def send_parts(t, items, sem):
        y = (x + t + 1) % nch
        tr = []
        for d, engines in items:
            jp = (j + d) % m
            slot = rx_slot(t, d)
            tr.append(RemoteDMATransfer(
                dst_ids=[dst_id(mem[x][jp])], dma_engine_mask=_mask(engines), remote_sem=sem,
                srcs=pieces(pos[(y, jp)]), dsts=[T.rx[:, B * slot:B * slot + B]], alu_op=1))
        g.remote_dma_fused(tr, local_sem=S.loc)
        return sum(len(e) for _d, e in items)

    def forward(t):
        y = (x + t + 1) % nch
        dest = mem[y][j]
        srcs = pieces(pos[(y, j)]) + [T.rx[:, B * s:B * s + B] for s in range(t * (m - 1), (t + 1) * (m - 1))]
        g.remote_dma_fused([RemoteDMATransfer(
            dst_ids=[dst_id(dest)], dma_engine_mask=_mask(off_e), remote_sem=S["o%d" % t],
            srcs=srcs, dsts=[T.rxo[:, B * t:B * t + B]], alu_op=1)], local_sem=S.loc)
        return len(off_e)

    gathered(3)
    n_rx0 = send_parts(0, [(d, quarter[d - 1]) for d in range(1, m)], S.rx0)
    gathered(5)
    n_rx1 = send_parts(1, [(1, on_only), (2, off_e)], S.rx1)
    gathered(6)
    n_rx1 += send_parts(1, [(3, on_all)], S.rx1)
    gathered(7)
    g.wait_ge(S.rx0, n_rx0)
    loc += forward(0)
    gathered(8)
    g.wait_ge(S.rx1, n_rx1)
    loc += forward(1)
    gathered(10)
    n_rx2 = send_parts(2, [(1, on_only[:half]), (2, on_only[half:])], S.rx2)
    gathered(11)
    n_rx3 = send_parts(2, [(3, on_only)], S.rx3)
    loc += n_rx0 + n_rx1 + n_rx2 + n_rx3

    acc = T.acc[:, 0:B]
    a_own, b_own, c_own, d_own = pieces(own)
    n = [0]

    def add(part):
        if n[0]:
            v.wait_ge(S.acc, n[0])
        v.tensor_tensor(acc, acc, part, AluOpType.add).then_inc(S.acc, 1)
        n[0] += 1

    v.wait_ge(S.cd, N)
    v.tensor_tensor(acc, c_own, d_own, AluOpType.add).then_inc(S.acc, 1)
    n[0] += 1
    v.wait_ge(S.ab, N)
    add(a_own)
    add(b_own)
    v.wait_ge(S.o0, len(off_e))
    add(T.rxo[:, 0:B])
    v.wait_ge(S.rx2, n_rx2)
    for d in (1, 2):
        s = rx_slot(2, d)
        add(T.rx[:, B * s:B * s + B])
    v.wait_ge(S.rx3, n_rx3)
    s = rx_slot(2, 3)
    add(T.rx[:, B * s:B * s + B])
    v.wait_ge(S.o1, len(off_e))
    v.wait_ge(S.acc, n[0])
    for q in range(4):
        v.tensor_tensor(T.ysb[:, 32 * q:32 * q + 32], T.acc[:, q:B:4], T.rxo[:, B + q:2 * B:4],
                        AluOpType.add).then_inc(S.fin, 1)
    g.sync.wait_ge(S.fin, 4)
    g.sync.dma_start(T.y[:, :], T.ysb[:, :]).then_inc(S.y, 16)
    g.sync.wait_ge(S.y, 16)
    g.wait_ge(S.loc, loc)
